import numpy as np
import ml_dtypes


def mxq(x, axis, fmt="e4m3"):
    dtype, down = {"e4m3": (ml_dtypes.float8_e4m3fn, 7), "e5m2": (ml_dtypes.float8_e5m2, 14)}[fmt]
    v = np.moveaxis(np.asarray(x, np.float32).astype(ml_dtypes.bfloat16).astype(np.float64), axis, -1)
    blocks = v.reshape(v.shape[:-1] + (-1, 32))
    amax = np.abs(blocks).max(-1, keepdims=True)
    byte = np.maximum(np.where(amax > 0, np.frexp(amax)[1] - 1 + 127, 0) - down, 1)
    scale = np.exp2(byte - 127.0)
    codes = (blocks / scale).astype(np.float32).astype(dtype).astype(np.float64)
    return np.moveaxis((codes * scale).reshape(v.shape), -1, axis)


WIDE = False


def mx_kscale(k):
    if not WIDE:
        return np.ones(k)
    levels = np.array([10, -10, 5, -5, 0])
    if k % 512:
        return np.exp2(np.random.permutation(np.resize(levels, k // 32))).repeat(32)
    a = np.empty((k // 512, 16))
    for p in range(k // 512):
        a[p, :8] = np.random.permutation(np.resize(levels, 8))
        for g in range(8):
            far = levels[np.abs(levels - a[p, g]) >= 10]
            a[p, g + 8] = far[np.random.randint(len(far))]
    return np.exp2(a.ravel()).repeat(32)


def f64(x):
    return np.asarray(x).astype(np.float64)


E2M1 = np.array([0.0, 0.5, 1.0, 1.5, 2.0, 3.0, 4.0, 6.0, -0.0, -0.5, -1.0, -1.5, -2.0, -3.0, -4.0, -6.0])


def pack_weight(w, fmt):
    k, n = w.shape
    w = f64(np.asarray(w, np.float32).astype(ml_dtypes.bfloat16)).reshape(k // 32, 32, n)
    amax = np.abs(w).max(1)
    if fmt == "e4m3":
        byte = np.frexp(amax)[1] - 1 + 127 - 7
    else:
        mant, ex = np.frexp(amax / 6.0)
        byte = np.where(mant > 0.5, ex, ex - 1) + 127
    byte = np.clip(np.where(amax > 0, byte, 1), 1, 254)
    scaled = (w * np.exp2(127.0 - byte)[:, None, :]).reshape(k, n).astype(np.float32)
    by_word = np.ascontiguousarray(scaled.reshape(k // 512, 128, 4, n).transpose(0, 1, 3, 2))
    if fmt == "e4m3":
        words = by_word.astype(ml_dtypes.float8_e4m3fn).view(np.uint8)
    else:
        c = by_word.astype(ml_dtypes.float4_e2m1fn).view(np.uint8) & 0xF
        words = (c[..., 0::2] | (c[..., 1::2] << 4)).reshape(k // 512, 128, 2 * n)
    return np.ascontiguousarray(words), np.ascontiguousarray(byte.astype(np.uint8).reshape(k // 512, 16, n))


def unpack_weight(words, scales, fmt):
    g, _, n = scales.shape
    words = np.ascontiguousarray(words).reshape(g, 128, n, -1)
    if fmt == "e4m3":
        vals = words.view(ml_dtypes.float8_e4m3fn).astype(np.float64)
    else:
        nib = np.empty((g, 128, n, 4), np.uint8)
        nib[..., 0::2] = words & 0xF
        nib[..., 1::2] = words >> 4
        vals = E2M1[nib]
    vals = vals * np.repeat(np.exp2(scales.astype(np.float64) - 127.0), 8, axis=1)[..., None]
    return vals.transpose(0, 1, 3, 2).reshape(g * 512, n)


K, M, T = 1024, 1024, 1024


def setup_inputs():
    n = np.random.standard_normal
    s = mx_kscale(K)[:, None]
    p_wr = pack_weight(n((K, M)) / np.sqrt(2 * K) / s, "e4m3")
    p_wi = pack_weight(n((K, M)) / np.sqrt(2 * K) / s, "e2m1")
    return {
        "xr": (n((K, T)) * s).astype(np.float32),
        "xi": (n((K, T)) * s).astype(np.float32),
        "wr_words": p_wr[0],
        "wr_scales": p_wr[1],
        "wi_words": p_wi[0],
        "wi_scales": p_wi[1],
    }


def reference(xr, xi, wr_words, wr_scales, wi_words, wi_scales):
    xr_ = mxq(f64(xr), 0, "e4m3")
    xi_ = mxq(f64(xi), 0, "e4m3")
    wr_ = unpack_weight(wr_words, wr_scales, "e4m3")
    wi_ = unpack_weight(wi_words, wi_scales, "e2m1")
    return xr_.T @ wr_ - xi_.T @ wi_, xi_.T @ wr_ + xr_.T @ wi_

@@ -1,0 +1,195 @@
+from contextlib import ExitStack
+
+import concourse.mybir as mybir
+
+K, M, T = 1024, 1024, 1024
+FLOPS = 4 * 2 * K * M * T
+
+F32 = mybir.dt.float32
+BF16 = mybir.dt.bfloat16
+I32 = mybir.dt.int32
+U32 = mybir.dt.uint32
+U8 = mybir.dt.uint8
+FP8X4 = mybir.dt.float8_e4m3fn_x4
+FP4X4 = mybir.dt.float4_e2m1fn_x4
+
+P = 128
+PACK = 4
+K_PASS = P * PACK
+PASSES = K // K_PASS
+T_TILE = 128
+N_HALF = 512
+HALVES = M // N_HALF
+BANKS = 8
+LINE = 4
+CHUNKS = ((0, 256), (256, 256), (512, 512))
+X_ORDER = (("xi", 0), ("xr", 0), ("xi", 1), ("xr", 1))
+STEPS = (
+    ("xi", "wr", 0, 1),
+    ("xr", "wr", 0, 0),
+    ("xr", "wi", 0, 1),
+    ("neg_xi", "wi", 0, 0),
+    ("xi", "wr", 1, 1),
+    ("neg_xi", "wi", 1, 0),
+    ("xr", "wr", 1, 0),
+    ("xr", "wi", 1, 1),
+)
+
+
+def tile_mix_cplx_tm_none_kernel(tc, xr, xi, wr_words, wr_scales, wi_words, wi_scales, out_0, out_1):
+    nc = tc.nc
+    x_hbm = {"xr": xr, "xi": xi}
+    outs = (out_0, out_1)
+
+    with ExitStack() as ctx:
+        keep = ctx.enter_context(tc.tile_pool(name="keep", bufs=1))
+        stage = ctx.enter_context(tc.tile_pool(name="stage", bufs=4))
+        psum = ctx.enter_context(tc.psum_pool(name="psum", bufs=1))
+        ctx.enter_context(tc.manual_schedule())
+
+        w_plane = {}
+        for name in ("wr", "wi"):
+            w_plane[name] = keep.tile([P, PASSES, M], U8, name=name + "_plane", align_bytes=64)
+            nc.vector.memset(w_plane[name][:].bitcast(I32), 0)
+
+        raw = {}
+        w_codes = {}
+
+        def load_x(name, a, chunk):
+            t0, width = CHUNKS[chunk]
+            tl = keep.tile([P, PACK, width], F32, name="raw_%s_%d_%d" % (name, a, chunk))
+            rows = x_hbm[name][a * K_PASS : (a + 1) * K_PASS, t0 : t0 + width]
+            nc.sync.dma_start(out=tl[:], in_=rows.rearrange("(p j) w -> p j w", j=PACK))
+            raw[name, a, chunk] = tl
+
+        def load_wr(a, h0, h1):
+            tl = keep.tile([P, (h1 - h0) * N_HALF], U32, name="wr_%d_%d" % (a, h0), align_bytes=64)
+            words = wr_words[a].rearrange("p n i -> p (n i)").bitcast(I32)
+            nc.sync.dma_start(out=tl[:].bitcast(I32), in_=words[:, h0 * N_HALF : h1 * N_HALF])
+            for h in range(h0, h1):
+                w_codes["wr", a, h] = tl[:, (h - h0) * N_HALF : (h - h0 + 1) * N_HALF].bitcast(FP8X4)
+
+        def load_wi(a):
+            tl = keep.tile([P, 2 * M], U8, name="wi_%d" % a, align_bytes=64)
+            nc.sync.dma_start(out=tl[:].bitcast(I32), in_=wi_words[a].bitcast(I32))
+            for h in range(HALVES):
+                w_codes["wi", a, h] = tl[:, 2 * h * N_HALF : 2 * (h + 1) * N_HALF].bitcast(FP4X4)
+
+        def load_scales(name, scales):
+            rows = scales.bitcast(I32).rearrange("a (q r) n -> r q a n", r=4)
+            for r in range(4):
+                nc.sync.dma_start(out=w_plane[name][r:P:32, :, :].bitcast(I32), in_=rows[r])
+
+        load_x("xi", 0, 0)
+        load_wr(0, 0, 1)
+        load_scales("wr", wr_scales)
+        load_wr(0, 1, 2)
+        load_x("xr", 0, 0)
+        load_scales("wi", wi_scales)
+        load_wi(0)
+        load_x("xi", 1, 0)
+        load_wr(1, 0, 2)
+        load_wi(1)
+        load_x("xr", 1, 0)
+        for chunk in range(1, len(CHUNKS)):
+            for name, a in X_ORDER:
+                load_x(name, a, chunk)
+
+        x_codes = {}
+        x_plane = {}
+
+        def quantize(name, a, tile, grouped):
+            codes = keep.tile([P, T_TILE], U32, name="codes_%s_%d_%d" % (name, a, tile), align_bytes=64)
+            plane = keep.tile([P, T_TILE], U8, name="plane_%s_%d_%d" % (name, a, tile), align_bytes=64)
+            nc.vector.quantize_mx(out=codes[:].bitcast(FP8X4), scales=plane[:], in_=grouped[:])
+            x_codes[name, a, tile] = codes[:].bitcast(FP8X4)
+            x_plane[name, a, tile] = plane[:]
+
+        def convert_pair(name, a, chunk, first_tile):
+            t0 = CHUNKS[chunk][0]
+            tiles = (first_tile, first_tile + 1)
+            grouped = {}
+            for tile in tiles:
+                grouped[tile] = stage.tile([P, T_TILE * PACK], BF16, name="grouped", align_bytes=64)
+                c0 = tile * T_TILE - t0
+                nc.vector.tensor_copy(
+                    out=grouped[tile][:].rearrange("p (c i j) -> p c j i", i=LINE, j=PACK),
+                    in_=raw[name, a, chunk][:, :, c0 : c0 + T_TILE].rearrange("p j (c i) -> p c j i", i=LINE),
+                )
+            for tile in tiles:
+                quantize(name, a, tile, grouped[tile])
+            if name == "xi":
+                negated = {}
+                for tile in tiles:
+                    negated[tile] = stage.tile([P, T_TILE * PACK], BF16, name="negated", align_bytes=64)
+                    nc.vector.tensor_scalar_mul(negated[tile][:], grouped[tile][:], -1.0)
+                for tile in tiles:
+                    quantize("neg_xi", a, tile, negated[tile])
+
+        for chunk in (0, 1):
+            for name, a in X_ORDER:
+                convert_pair(name, a, chunk, 2 * chunk)
+        convert_pair("xi", 0, 2, 4)
+        convert_pair("xi", 0, 2, 6)
+        for first_tile in (4, 6):
+            for name, a in X_ORDER[1:]:
+                convert_pair(name, a, 2, first_tile)
+
+        free_banks = list(range(BANKS))
+        acc = {}
+        done = {}
+        result = {}
+
+        def multiply(tile, step, h):
+            x_name, w_name, a, o = step
+            key = (tile, o, h)
+            if key not in acc:
+                bank = free_banks.pop(0)
+                acc[key] = (bank, psum.tile([T_TILE, N_HALF], F32, name="bank_%d" % bank))
+                done[key] = 0
+            done[key] = done[key] + 1
+            last = done[key] == 2 * PASSES
+            nc.tensor.matmul_mx(
+                out=acc[key][1][:],
+                lhsT=x_codes[x_name, a, tile],
+                lhsT_scale=x_plane[x_name, a, tile],
+                rhs=w_codes[w_name, a, h],
+                rhs_scale=w_plane[w_name][:, a, h * N_HALF : (h + 1) * N_HALF],
+                start=done[key] == 1,
+                stop=last,
+            )
+            if last:
+                drain(tile, o, h)
+
+        def drain(tile, o, h):
+            bank, sums = acc[tile, o, h]
+            if (tile, o) not in result:
+                result[tile, o] = keep.tile([T_TILE, M], F32, name="result_%d_%d" % (tile, o))
+            cols = slice(h * N_HALF, (h + 1) * N_HALF)
+            rows = slice(tile * T_TILE, (tile + 1) * T_TILE)
+            nc.scalar.copy(out=result[tile, o][:, cols], in_=sums[:])
+            free_banks.append(bank)
+            if tile == T // T_TILE - 1:
+                nc.sync.dma_start(out=outs[o][rows, cols], in_=result[tile, o][:, cols])
+            elif h == HALVES - 1:
+                nc.sync.dma_start(out=outs[o][rows, :], in_=result[tile, o][:])
+
+        for step in STEPS[:-2]:
+            for h in range(HALVES):
+                for tile in (0, 1):
+                    multiply(tile, step, h)
+        for tile in (0, 1):
+            for step in STEPS[-2:]:
+                for h in range(HALVES):
+                    multiply(tile, step, h)
+        for tile in range(2, T // T_TILE):
+            if tile in (2, 4):
+                for step in STEPS:
+                    for h in range(HALVES):
+                        multiply(tile, step, h)
+            else:
+                for o in range(2):
+                    for h in range(HALVES):
+                        for step in STEPS:
+                            if step[3] == o:
+                                multiply(tile, step, h)

@@ -18,11 +18,13 @@ PACK = 4
 K_PASS = P * PACK
 PASSES = K // K_PASS
 T_TILE = 128
-N_HALF = 512
-HALVES = M // N_HALF
+T_PAIR = 2 * T_TILE
+PAIRS = T // T_PAIR
+N_BANK = 512
+N_TAIL = 256
+N_FP4_NARROW = 128
 BANKS = 8
-LINE = 4
-CHUNKS = ((0, 256), (256, 256), (512, 512))
+PLANE_START = {"wr": 4, "wi": 0}
 X_ORDER = (("xi", 0), ("xr", 0), ("xi", 1), ("xr", 1))
 STEPS = (
     ("xi", "wr", 0, 1),
@@ -48,52 +50,57 @@ def tile_mix_cplx_tm_none_kernel(tc, xr, xi, wr_words, wr_scales, wi_words, wi_s
         ctx.enter_context(tc.manual_schedule())
 
         w_plane = {}
-        for name in ("wr", "wi"):
+        for name, engine in (("wi", nc.gpsimd), ("wr", nc.vector)):
             w_plane[name] = keep.tile([P, PASSES, M], U8, name=name + "_plane", align_bytes=64)
-            nc.vector.memset(w_plane[name][:].bitcast(I32), 0)
+            engine.memset(w_plane[name][:].bitcast(I32), 0)
 
         raw = {}
         w_codes = {}
 
-        def load_x(name, a, chunk):
-            t0, width = CHUNKS[chunk]
-            tl = keep.tile([P, PACK, width], F32, name="raw_%s_%d_%d" % (name, a, chunk))
+        def load_x(name, a, first_pair, pairs):
+            t0, width = first_pair * T_PAIR, pairs * T_PAIR
+            tl = keep.tile([P, PACK, width], F32, name="raw_%s_%d_%d" % (name, a, first_pair))
             rows = x_hbm[name][a * K_PASS : (a + 1) * K_PASS, t0 : t0 + width]
             nc.sync.dma_start(out=tl[:], in_=rows.rearrange("(p j) w -> p j w", j=PACK))
-            raw[name, a, chunk] = tl
+            for g in range(pairs):
+                raw[name, a, first_pair + g] = tl[:, :, g * T_PAIR : (g + 1) * T_PAIR]
 
-        def load_wr(a, h0, h1):
-            tl = keep.tile([P, (h1 - h0) * N_HALF], U32, name="wr_%d_%d" % (a, h0), align_bytes=64)
+        def load_wr(a, n0, n1):
+            tl = keep.tile([P, n1 - n0], U32, name="wr_%d_%d" % (a, n0), align_bytes=64)
             words = wr_words[a].rearrange("p n i -> p (n i)").bitcast(I32)
-            nc.sync.dma_start(out=tl[:].bitcast(I32), in_=words[:, h0 * N_HALF : h1 * N_HALF])
-            for h in range(h0, h1):
-                w_codes["wr", a, h] = tl[:, (h - h0) * N_HALF : (h - h0 + 1) * N_HALF].bitcast(FP8X4)
+            nc.sync.dma_start(out=tl[:].bitcast(I32), in_=words[:, n0:n1])
+            for n in range(n0, n1, N_BANK):
+                w_codes["wr", a, n] = (tl, n0)
 
         def load_wi(a):
             tl = keep.tile([P, 2 * M], U8, name="wi_%d" % a, align_bytes=64)
             nc.sync.dma_start(out=tl[:].bitcast(I32), in_=wi_words[a].bitcast(I32))
-            for h in range(HALVES):
-                w_codes["wi", a, h] = tl[:, 2 * h * N_HALF : 2 * (h + 1) * N_HALF].bitcast(FP4X4)
+            for n in range(0, M, N_BANK):
+                w_codes["wi", a, n] = (tl, 0)
 
-        def load_scales(name, scales):
+        def load_scales(name, scales, queue):
             rows = scales.bitcast(I32).rearrange("a (q r) n -> r q a n", r=4)
             for r in range(4):
-                nc.sync.dma_start(out=w_plane[name][r:P:32, :, :].bitcast(I32), in_=rows[r])
+                first = PLANE_START[name] + r
+                queue.dma_start(out=w_plane[name][first:P:32, :, :].bitcast(I32), in_=rows[r])
 
-        load_x("xi", 0, 0)
-        load_wr(0, 0, 1)
-        load_scales("wr", wr_scales)
-        load_wr(0, 1, 2)
-        load_x("xr", 0, 0)
-        load_scales("wi", wi_scales)
+        load_scales("wi", wi_scales, nc.gpsimd)
+        load_x("xi", 0, 0, 1)
+        load_wr(0, 0, N_BANK)
+        load_scales("wr", wr_scales, nc.sync)
+        load_wr(0, N_BANK, M)
+        load_x("xr", 0, 0, 1)
         load_wi(0)
-        load_x("xi", 1, 0)
-        load_wr(1, 0, 2)
+        load_x("xi", 1, 0, 1)
+        load_wr(1, 0, M)
         load_wi(1)
-        load_x("xr", 1, 0)
-        for chunk in range(1, len(CHUNKS)):
-            for name, a in X_ORDER:
-                load_x(name, a, chunk)
+        load_x("xr", 1, 0, 1)
+        for name, a in X_ORDER:
+            load_x(name, a, 1, 1)
+        for name, a in X_ORDER[:-1]:
+            load_x(name, a, 2, 2)
+        for pair in (2, 3):
+            load_x("xr", 1, pair, 1)
 
         x_codes = {}
         x_plane = {}
@@ -105,91 +112,108 @@ def tile_mix_cplx_tm_none_kernel(tc, xr, xi, wr_words, wr_scales, wi_words, wi_s
             x_codes[name, a, tile] = codes[:].bitcast(FP8X4)
             x_plane[name, a, tile] = plane[:]
 
-        def convert_pair(name, a, chunk, first_tile):
-            t0 = CHUNKS[chunk][0]
-            tiles = (first_tile, first_tile + 1)
-            grouped = {}
-            for tile in tiles:
-                grouped[tile] = stage.tile([P, T_TILE * PACK], BF16, name="grouped", align_bytes=64)
-                c0 = tile * T_TILE - t0
+        def convert_pair(name, a, pair):
+            grouped = []
+            source = raw[name, a, pair].rearrange("p j (c i e) -> p e c j i", i=2, e=2)
+            for e in range(2):
+                grouped.append(stage.tile([P, T_TILE * PACK], BF16, name="grouped", align_bytes=64))
                 nc.vector.tensor_copy(
-                    out=grouped[tile][:].rearrange("p (c i j) -> p c j i", i=LINE, j=PACK),
-                    in_=raw[name, a, chunk][:, :, c0 : c0 + T_TILE].rearrange("p j (c i) -> p c j i", i=LINE),
+                    out=grouped[e][:].rearrange("p (c i j) -> p c j i", i=2, j=PACK),
+                    in_=source[:, e],
                 )
-            for tile in tiles:
-                quantize(name, a, tile, grouped[tile])
+            for e in range(2):
+                quantize(name, a, 2 * pair + e, grouped[e])
             if name == "xi":
-                negated = {}
-                for tile in tiles:
-                    negated[tile] = stage.tile([P, T_TILE * PACK], BF16, name="negated", align_bytes=64)
-                    nc.vector.tensor_scalar_mul(negated[tile][:], grouped[tile][:], -1.0)
-                for tile in tiles:
-                    quantize("neg_xi", a, tile, negated[tile])
+                negated = []
+                for e in range(2):
+                    negated.append(stage.tile([P, T_TILE * PACK], BF16, name="negated", align_bytes=64))
+                    nc.vector.tensor_scalar_mul(negated[e][:], grouped[e][:], -1.0)
+                for e in range(2):
+                    quantize("neg_xi", a, 2 * pair + e, negated[e])
 
-        for chunk in (0, 1):
+        for pair in (0, 1):
             for name, a in X_ORDER:
-                convert_pair(name, a, chunk, 2 * chunk)
-        convert_pair("xi", 0, 2, 4)
-        convert_pair("xi", 0, 2, 6)
-        for first_tile in (4, 6):
+                convert_pair(name, a, pair)
+        convert_pair("xi", 0, 2)
+        convert_pair("xi", 0, 3)
+        for pair in (2, 3):
             for name, a in X_ORDER[1:]:
-                convert_pair(name, a, 2, first_tile)
+                convert_pair(name, a, pair)
 
         free_banks = list(range(BANKS))
         acc = {}
         done = {}
         result = {}
 
-        def multiply(tile, step, h):
+        def multiply(tile, step, n0, width):
             x_name, w_name, a, o = step
-            key = (tile, o, h)
+            key = (tile, o, n0)
             if key not in acc:
                 bank = free_banks.pop(0)
-                acc[key] = (bank, psum.tile([T_TILE, N_HALF], F32, name="bank_%d" % bank))
+                acc[key] = (bank, psum.tile([T_TILE, width], F32, name="bank_%d" % bank))
                 done[key] = 0
             done[key] = done[key] + 1
             last = done[key] == 2 * PASSES
-            nc.tensor.matmul_mx(
-                out=acc[key][1][:],
-                lhsT=x_codes[x_name, a, tile],
-                lhsT_scale=x_plane[x_name, a, tile],
-                rhs=w_codes[w_name, a, h],
-                rhs_scale=w_plane[w_name][:, a, h * N_HALF : (h + 1) * N_HALF],
-                start=done[key] == 1,
-                stop=last,
-            )
+            w_tile, w_n0 = w_codes[w_name, a, n0 - n0 % N_BANK]
+            n_step = N_FP4_NARROW if w_name == "wi" and width < N_BANK else width
+            for n in range(n0, n0 + width, n_step):
+                if w_name == "wr":
+                    moving = w_tile[:, n - w_n0 : n - w_n0 + n_step].bitcast(FP8X4)
+                else:
+                    moving = w_tile[:, 2 * n : 2 * (n + n_step)].bitcast(FP4X4)
+                nc.tensor.matmul_mx(
+                    out=acc[key][1][:, n - n0 : n - n0 + n_step],
+                    lhsT=x_codes[x_name, a, tile],
+                    lhsT_scale=x_plane[x_name, a, tile],
+                    rhs=moving,
+                    rhs_scale=w_plane[w_name][PLANE_START[w_name] :, a, n : n + n_step],
+                    start=done[key] == 1,
+                    stop=last,
+                )
             if last:
-                drain(tile, o, h)
+                drain(tile, o, n0, width)
 
-        def drain(tile, o, h):
-            bank, sums = acc[tile, o, h]
-            if (tile, o) not in result:
-                result[tile, o] = keep.tile([T_TILE, M], F32, name="result_%d_%d" % (tile, o))
-            cols = slice(h * N_HALF, (h + 1) * N_HALF)
-            rows = slice(tile * T_TILE, (tile + 1) * T_TILE)
-            nc.scalar.copy(out=result[tile, o][:, cols], in_=sums[:])
+        def drain(tile, o, n0, width):
+            bank, sums = acc[tile, o, n0]
+            pair, e = divmod(tile, 2)
+            if (pair, o) not in result:
+                result[pair, o] = keep.tile([T_TILE, 2, M], F32, name="result_%d_%d" % (pair, o))
+            held = result[pair, o]
+            nc.scalar.copy(out=held[:, e, n0 : n0 + width], in_=sums[:])
             free_banks.append(bank)
-            if tile == T // T_TILE - 1:
-                nc.sync.dma_start(out=outs[o][rows, cols], in_=result[tile, o][:, cols])
-            elif h == HALVES - 1:
-                nc.sync.dma_start(out=outs[o][rows, :], in_=result[tile, o][:])
+            rows = outs[o][pair * T_PAIR : (pair + 1) * T_PAIR, :].rearrange("(m e) n -> m e n", e=2)
+            row_complete = n0 + width == M
+            if pair < PAIRS - 1:
+                if e == 1 and row_complete:
+                    nc.sync.dma_start(out=rows, in_=held[:])
+            elif e == 1 and o == 1:
+                nc.sync.dma_start(out=rows[:, e, n0 : n0 + width], in_=held[:, e, n0 : n0 + width])
+            elif row_complete:
+                nc.sync.dma_start(out=rows[:, e, :], in_=held[:, e, :])
 
+        halves = range(0, M, N_BANK)
         for step in STEPS[:-2]:
-            for h in range(HALVES):
+            for n0 in halves:
                 for tile in (0, 1):
-                    multiply(tile, step, h)
+                    multiply(tile, step, n0, N_BANK)
         for tile in (0, 1):
             for step in STEPS[-2:]:
-                for h in range(HALVES):
-                    multiply(tile, step, h)
-        for tile in range(2, T // T_TILE):
+                for n0 in halves:
+                    multiply(tile, step, n0, N_BANK)
+        last_tile = T // T_TILE - 1
+        for tile in range(2, last_tile + 1):
             if tile in (2, 4):
                 for step in STEPS:
-                    for h in range(HALVES):
-                        multiply(tile, step, h)
+                    for n0 in halves:
+                        multiply(tile, step, n0, N_BANK)
             else:
                 for o in range(2):
-                    for h in range(HALVES):
-                        for step in STEPS:
-                            if step[3] == o:
-                                multiply(tile, step, h)
+                    steps = [step for step in STEPS if step[3] == o]
+                    for n0 in halves:
+                        if (tile, o, n0) == (last_tile, 1, M - N_BANK):
+                            for n1 in range(n0, M, N_TAIL):
+                                for step in steps[:2] + steps[:1:-1]:
+                                    multiply(tile, step, n1, N_TAIL)
+                        else:
+                            for step in steps:
+                                multiply(tile, step, n0, N_BANK)

@@ -29,12 +29,12 @@ X_ORDER = (("xi", 0), ("xr", 0), ("xi", 1), ("xr", 1))
 STEPS = (
     ("xi", "wr", 0, 1),
     ("xr", "wr", 0, 0),
-    ("xr", "wi", 0, 1),
     ("neg_xi", "wi", 0, 0),
-    ("xi", "wr", 1, 1),
+    ("xr", "wi", 0, 1),
     ("neg_xi", "wi", 1, 0),
-    ("xr", "wr", 1, 0),
     ("xr", "wi", 1, 1),
+    ("xi", "wr", 1, 1),
+    ("xr", "wr", 1, 0),
 )
 
 
@@ -92,9 +92,9 @@ def tile_mix_cplx_tm_none_kernel(tc, xr, xi, wr_words, wr_scales, wi_words, wi_s
         load_x("xr", 0, 0, 1)
         load_wi(0)
         load_x("xi", 1, 0, 1)
-        load_wr(1, 0, M)
         load_wi(1)
         load_x("xr", 1, 0, 1)
+        load_wr(1, 0, M)
         for name, a in X_ORDER:
             load_x(name, a, 1, 1)
         for name, a in X_ORDER[:-1]:
@@ -113,11 +113,12 @@ def tile_mix_cplx_tm_none_kernel(tc, xr, xi, wr_words, wr_scales, wi_words, wi_s
             x_plane[name, a, tile] = plane[:]
 
         def convert_pair(name, a, pair):
+            second_copy = nc.scalar.copy if pair == 0 else nc.vector.tensor_copy
             grouped = []
             source = raw[name, a, pair].rearrange("p j (c i e) -> p e c j i", i=2, e=2)
             for e in range(2):
                 grouped.append(stage.tile([P, T_TILE * PACK], BF16, name="grouped", align_bytes=64))
-                nc.vector.tensor_copy(
+                (nc.vector.tensor_copy, second_copy)[e](
                     out=grouped[e][:].rearrange("p (c i j) -> p c j i", i=2, j=PACK),
                     in_=source[:, e],
                 )
@@ -167,8 +168,8 @@ def tile_mix_cplx_tm_none_kernel(tc, xr, xi, wr_words, wr_scales, wi_words, wi_s
                     lhsT_scale=x_plane[x_name, a, tile],
                     rhs=moving,
                     rhs_scale=w_plane[w_name][PLANE_START[w_name] :, a, n : n + n_step],
-                    start=done[key] == 1,
-                    stop=last,
+                    start=done[key] == 1 and n == n0,
+                    stop=last and n + n_step == n0 + width,
                 )
             if last:
                 drain(tile, o, n0, width)
@@ -206,14 +207,14 @@ def tile_mix_cplx_tm_none_kernel(tc, xr, xi, wr_words, wr_scales, wi_words, wi_s
                 for step in STEPS:
                     for n0 in halves:
                         multiply(tile, step, n0, N_BANK)
-            else:
-                for o in range(2):
-                    steps = [step for step in STEPS if step[3] == o]
-                    for n0 in halves:
-                        if (tile, o, n0) == (last_tile, 1, M - N_BANK):
-                            for n1 in range(n0, M, N_TAIL):
-                                for step in steps[:2] + steps[:1:-1]:
-                                    multiply(tile, step, n1, N_TAIL)
-                        else:
-                            for step in steps:
-                                multiply(tile, step, n0, N_BANK)
+                continue
+            runs = [[(o, n0, N_BANK) for n0 in halves] for o in range(2)]
+            if tile == last_tile:
+                narrow = [(1, n0, N_TAIL) for n0 in range(M - N_BANK, M, N_TAIL)]
+                runs = [[group] for group in runs[0] + runs[1][:-1] + narrow]
+            for i, run in enumerate(runs):
+                for w_name in ("wi", "wr") if i % 2 else ("wr", "wi"):
+                    for o, n0, width in run:
+                        for step in STEPS:
+                            if step[1] == w_name and step[3] == o:
+                                multiply(tile, step, n0, width)

from contextlib import ExitStack

import concourse.mybir as mybir

K, M, T = 1024, 1024, 1024
FLOPS = 4 * 2 * K * M * T

F32 = mybir.dt.float32
BF16 = mybir.dt.bfloat16
I32 = mybir.dt.int32
U32 = mybir.dt.uint32
U8 = mybir.dt.uint8
FP8X4 = mybir.dt.float8_e4m3fn_x4
FP4X4 = mybir.dt.float4_e2m1fn_x4

P = 128
PACK = 4
K_PASS = P * PACK
PASSES = K // K_PASS
T_TILE = 128
T_PAIR = 2 * T_TILE
PAIRS = T // T_PAIR
N_BANK = 512
N_TAIL = 256
N_FP4_NARROW = 128
BANKS = 8
PLANE_START = {"wr": 4, "wi": 0}
X_ORDER = (("xi", 0), ("xr", 0), ("xi", 1), ("xr", 1))
STEPS = (
    ("xi", "wr", 0, 1),
    ("xr", "wr", 0, 0),
    ("neg_xi", "wi", 0, 0),
    ("xr", "wi", 0, 1),
    ("neg_xi", "wi", 1, 0),
    ("xr", "wi", 1, 1),
    ("xi", "wr", 1, 1),
    ("xr", "wr", 1, 0),
)


def tile_mix_cplx_tm_none_kernel(tc, xr, xi, wr_words, wr_scales, wi_words, wi_scales, out_0, out_1):
    nc = tc.nc
    x_hbm = {"xr": xr, "xi": xi}
    outs = (out_0, out_1)

    with ExitStack() as ctx:
        keep = ctx.enter_context(tc.tile_pool(name="keep", bufs=1))
        stage = ctx.enter_context(tc.tile_pool(name="stage", bufs=4))
        psum = ctx.enter_context(tc.psum_pool(name="psum", bufs=1))
        ctx.enter_context(tc.manual_schedule())

        w_plane = {}
        for name, engine in (("wi", nc.gpsimd), ("wr", nc.vector)):
            w_plane[name] = keep.tile([P, PASSES, M], U8, name=name + "_plane", align_bytes=64)
            engine.memset(w_plane[name][:].bitcast(I32), 0)

        raw = {}
        w_codes = {}

        def load_x(name, a, first_pair, pairs):
            t0, width = first_pair * T_PAIR, pairs * T_PAIR
            tl = keep.tile([P, PACK, width], F32, name="raw_%s_%d_%d" % (name, a, first_pair))
            rows = x_hbm[name][a * K_PASS : (a + 1) * K_PASS, t0 : t0 + width]
            nc.sync.dma_start(out=tl[:], in_=rows.rearrange("(p j) w -> p j w", j=PACK))
            for g in range(pairs):
                raw[name, a, first_pair + g] = tl[:, :, g * T_PAIR : (g + 1) * T_PAIR]

        def load_wr(a, n0, n1):
            tl = keep.tile([P, n1 - n0], U32, name="wr_%d_%d" % (a, n0), align_bytes=64)
            words = wr_words[a].rearrange("p n i -> p (n i)").bitcast(I32)
            nc.sync.dma_start(out=tl[:].bitcast(I32), in_=words[:, n0:n1])
            for n in range(n0, n1, N_BANK):
                w_codes["wr", a, n] = (tl, n0)

        def load_wi(a):
            tl = keep.tile([P, 2 * M], U8, name="wi_%d" % a, align_bytes=64)
            nc.sync.dma_start(out=tl[:].bitcast(I32), in_=wi_words[a].bitcast(I32))
            for n in range(0, M, N_BANK):
                w_codes["wi", a, n] = (tl, 0)

        def load_scales(name, scales, queue):
            rows = scales.bitcast(I32).rearrange("a (q r) n -> r q a n", r=4)
            for r in range(4):
                first = PLANE_START[name] + r
                queue.dma_start(out=w_plane[name][first:P:32, :, :].bitcast(I32), in_=rows[r])

        load_scales("wi", wi_scales, nc.gpsimd)
        load_x("xi", 0, 0, 1)
        load_wr(0, 0, N_BANK)
        load_scales("wr", wr_scales, nc.sync)
        load_wr(0, N_BANK, M)
        load_x("xr", 0, 0, 1)
        load_wi(0)
        load_x("xi", 1, 0, 1)
        load_wi(1)
        load_x("xr", 1, 0, 1)
        load_wr(1, 0, M)
        for name, a in X_ORDER:
            load_x(name, a, 1, 1)
        for name, a in X_ORDER[:-1]:
            load_x(name, a, 2, 2)
        for pair in (2, 3):
            load_x("xr", 1, pair, 1)

        x_codes = {}
        x_plane = {}

        def quantize(name, a, tile, grouped):
            codes = keep.tile([P, T_TILE], U32, name="codes_%s_%d_%d" % (name, a, tile), align_bytes=64)
            plane = keep.tile([P, T_TILE], U8, name="plane_%s_%d_%d" % (name, a, tile), align_bytes=64)
            nc.vector.quantize_mx(out=codes[:].bitcast(FP8X4), scales=plane[:], in_=grouped[:])
            x_codes[name, a, tile] = codes[:].bitcast(FP8X4)
            x_plane[name, a, tile] = plane[:]

        def convert_pair(name, a, pair):
            second_copy = nc.scalar.copy if pair == 0 else nc.vector.tensor_copy
            grouped = []
            source = raw[name, a, pair].rearrange("p j (c i e) -> p e c j i", i=2, e=2)
            for e in range(2):
                grouped.append(stage.tile([P, T_TILE * PACK], BF16, name="grouped", align_bytes=64))
                (nc.vector.tensor_copy, second_copy)[e](
                    out=grouped[e][:].rearrange("p (c i j) -> p c j i", i=2, j=PACK),
                    in_=source[:, e],
                )
            for e in range(2):
                quantize(name, a, 2 * pair + e, grouped[e])
            if name == "xi":
                negated = []
                for e in range(2):
                    negated.append(stage.tile([P, T_TILE * PACK], BF16, name="negated", align_bytes=64))
                    nc.vector.tensor_scalar_mul(negated[e][:], grouped[e][:], -1.0)
                for e in range(2):
                    quantize("neg_xi", a, 2 * pair + e, negated[e])

        for pair in (0, 1):
            for name, a in X_ORDER:
                convert_pair(name, a, pair)
        convert_pair("xi", 0, 2)
        convert_pair("xi", 0, 3)
        for pair in (2, 3):
            for name, a in X_ORDER[1:]:
                convert_pair(name, a, pair)

        free_banks = list(range(BANKS))
        acc = {}
        done = {}
        result = {}

        def multiply(tile, step, n0, width):
            x_name, w_name, a, o = step
            key = (tile, o, n0)
            if key not in acc:
                bank = free_banks.pop(0)
                acc[key] = (bank, psum.tile([T_TILE, width], F32, name="bank_%d" % bank))
                done[key] = 0
            done[key] = done[key] + 1
            last = done[key] == 2 * PASSES
            w_tile, w_n0 = w_codes[w_name, a, n0 - n0 % N_BANK]
            n_step = N_FP4_NARROW if w_name == "wi" and width < N_BANK else width
            for n in range(n0, n0 + width, n_step):
                if w_name == "wr":
                    moving = w_tile[:, n - w_n0 : n - w_n0 + n_step].bitcast(FP8X4)
                else:
                    moving = w_tile[:, 2 * n : 2 * (n + n_step)].bitcast(FP4X4)
                nc.tensor.matmul_mx(
                    out=acc[key][1][:, n - n0 : n - n0 + n_step],
                    lhsT=x_codes[x_name, a, tile],
                    lhsT_scale=x_plane[x_name, a, tile],
                    rhs=moving,
                    rhs_scale=w_plane[w_name][PLANE_START[w_name] :, a, n : n + n_step],
                    start=done[key] == 1 and n == n0,
                    stop=last and n + n_step == n0 + width,
                )
            if last:
                drain(tile, o, n0, width)

        def drain(tile, o, n0, width):
            bank, sums = acc[tile, o, n0]
            pair, e = divmod(tile, 2)
            if (pair, o) not in result:
                result[pair, o] = keep.tile([T_TILE, 2, M], F32, name="result_%d_%d" % (pair, o))
            held = result[pair, o]
            nc.scalar.copy(out=held[:, e, n0 : n0 + width], in_=sums[:])
            free_banks.append(bank)
            rows = outs[o][pair * T_PAIR : (pair + 1) * T_PAIR, :].rearrange("(m e) n -> m e n", e=2)
            row_complete = n0 + width == M
            if pair < PAIRS - 1:
                if e == 1 and row_complete:
                    nc.sync.dma_start(out=rows, in_=held[:])
            elif e == 1 and o == 1:
                nc.sync.dma_start(out=rows[:, e, n0 : n0 + width], in_=held[:, e, n0 : n0 + width])
            elif row_complete:
                nc.sync.dma_start(out=rows[:, e, :], in_=held[:, e, :])

        halves = range(0, M, N_BANK)
        for step in STEPS[:-2]:
            for n0 in halves:
                for tile in (0, 1):
                    multiply(tile, step, n0, N_BANK)
        for tile in (0, 1):
            for step in STEPS[-2:]:
                for n0 in halves:
                    multiply(tile, step, n0, N_BANK)
        last_tile = T // T_TILE - 1
        for tile in range(2, last_tile + 1):
            if tile in (2, 4):
                for step in STEPS:
                    for n0 in halves:
                        multiply(tile, step, n0, N_BANK)
                continue
            runs = [[(o, n0, N_BANK) for n0 in halves] for o in range(2)]
            if tile == last_tile:
                narrow = [(1, n0, N_TAIL) for n0 in range(M - N_BANK, M, N_TAIL)]
                runs = [[group] for group in runs[0] + runs[1][:-1] + narrow]
            for i, run in enumerate(runs):
                for w_name in ("wi", "wr") if i % 2 else ("wr", "wi"):
                    for o, n0, width in run:
                        for step in STEPS:
                            if step[1] == w_name and step[3] == o:
                                multiply(tile, step, n0, width)
